import numpy as np
import ml_dtypes


def mxq(x, axis, fmt="e4m3"):
    dtype, down = {"e4m3": (ml_dtypes.float8_e4m3fn, 7), "e5m2": (ml_dtypes.float8_e5m2, 14)}[fmt]
    v = np.moveaxis(np.asarray(x, np.float32).astype(ml_dtypes.bfloat16).astype(np.float64), axis, -1)
    blocks = v.reshape(v.shape[:-1] + (-1, 32))
    amax = np.abs(blocks).max(-1, keepdims=True)
    byte = np.maximum(np.where(amax > 0, np.frexp(amax)[1] - 1 + 127, 0) - down, 1)
    scale = np.exp2(byte - 127.0)
    codes = (blocks / scale).astype(np.float32).astype(dtype).astype(np.float64)
    return np.moveaxis((codes * scale).reshape(v.shape), -1, axis)


WIDE = False


def mx_kscale(k):
    if not WIDE:
        return np.ones(k)
    levels = np.array([10, -10, 5, -5, 0])
    if k % 512:
        return np.exp2(np.random.permutation(np.resize(levels, k // 32))).repeat(32)
    a = np.empty((k // 512, 16))
    for p in range(k // 512):
        a[p, :8] = np.random.permutation(np.resize(levels, 8))
        for g in range(8):
            far = levels[np.abs(levels - a[p, g]) >= 10]
            a[p, g + 8] = far[np.random.randint(len(far))]
    return np.exp2(a.ravel()).repeat(32)


def f64(x):
    return np.asarray(x).astype(np.float64)


def striped(idx):
    return np.tile(idx.reshape(-1, 16).T, (8, 1)).astype(np.uint16)


def unstriped(offs):
    return offs[:16].T.reshape(-1).astype(np.int64)


E2M1 = np.array([0.0, 0.5, 1.0, 1.5, 2.0, 3.0, 4.0, 6.0, -0.0, -0.5, -1.0, -1.5, -2.0, -3.0, -4.0, -6.0])


def pack_weight(w, fmt):
    k, n = w.shape
    w = f64(np.asarray(w, np.float32).astype(ml_dtypes.bfloat16)).reshape(k // 32, 32, n)
    amax = np.abs(w).max(1)
    if fmt == "e4m3":
        byte = np.frexp(amax)[1] - 1 + 127 - 7
    else:
        mant, ex = np.frexp(amax / 6.0)
        byte = np.where(mant > 0.5, ex, ex - 1) + 127
    byte = np.clip(np.where(amax > 0, byte, 1), 1, 254)
    scaled = (w * np.exp2(127.0 - byte)[:, None, :]).reshape(k, n).astype(np.float32)
    by_word = np.ascontiguousarray(scaled.reshape(k // 512, 128, 4, n).transpose(0, 1, 3, 2))
    if fmt == "e4m3":
        words = by_word.astype(ml_dtypes.float8_e4m3fn).view(np.uint8)
    else:
        c = by_word.astype(ml_dtypes.float4_e2m1fn).view(np.uint8) & 0xF
        words = (c[..., 0::2] | (c[..., 1::2] << 4)).reshape(k // 512, 128, 2 * n)
    return np.ascontiguousarray(words), np.ascontiguousarray(byte.astype(np.uint8).reshape(k // 512, 16, n))


def unpack_weight(words, scales, fmt):
    g, _, n = scales.shape
    words = np.ascontiguousarray(words).reshape(g, 128, n, -1)
    if fmt == "e4m3":
        vals = words.view(ml_dtypes.float8_e4m3fn).astype(np.float64)
    else:
        nib = np.empty((g, 128, n, 4), np.uint8)
        nib[..., 0::2] = words & 0xF
        nib[..., 1::2] = words >> 4
        vals = E2M1[nib]
    vals = vals * np.repeat(np.exp2(scales.astype(np.float64) - 127.0), 8, axis=1)[..., None]
    return vals.transpose(0, 1, 3, 2).reshape(g * 512, n)


def gelu(v):
    return 0.5 * v * (1.0 + np.tanh(np.sqrt(2.0 / np.pi) * (v + 0.044715 * v**3)))


def striped8(idx):
    return np.concatenate([v.reshape(-1, 16).T for v in idx]).astype(np.uint16)


def unstriped8(offs):
    return np.stack([offs[16 * g:16 * g + 16].T.reshape(-1) for g in range(8)]).astype(np.int64)


def heads(h, wgt, idx8):
    r = np.arange(h.shape[0])
    return wgt[r // 4 % 128] * h[r[:, None], idx8[r % 512 // 64]]


K, T, S, H, T2, P, N = 1024, 2048, 512, 1024, 1024, 512, 512

def setup_inputs():
    n = np.random.standard_normal
    s = mx_kscale(K)[:, None]
    u = mx_kscale(H)[:, None]
    tab_words, tab_scales = pack_weight(n((K, T)) * s, "e4m3")
    w1 = (0.6 * n((K, H)) / np.sqrt(K) / s).astype(np.float32)
    w2_words, w2_scales = pack_weight(0.42 * n((K, H)) / np.sqrt(K) / s, "e4m3")
    w3 = (n((H, N)) / np.sqrt(H) / u).astype(np.float32)
    w4_words, w4_scales = pack_weight(0.8 * n((K, N)) / np.sqrt(K) / s, "e2m1")
    phase = np.random.uniform(-0.6, 0.6, H).astype(np.float32)
    gain = (np.exp(0.3 * n(H)) * u[:, 0]).astype(np.float32)
    page0 = (0.8 * n((H, T2)) * u).astype(np.float32)
    wgs = np.exp(0.3 * n((128, S))).astype(np.float32)
    wgt = np.repeat(np.random.uniform(0.5, 2.0, (8, P)), 16, axis=0).astype(np.float32)
    offs = striped(np.random.permutation(T)[:S])
    offs2 = striped(np.random.permutation(T2)[:S])
    offs3 = striped8(np.stack([np.random.permutation(T2)[:P] for _ in range(8)]))
    return {"tab_words": tab_words, "tab_scales": tab_scales, "offs": offs, "w1": w1,
            "w2_words": w2_words, "w2_scales": w2_scales, "phase": phase, "gain": gain,
            "page0": page0, "wgs": wgs, "offs2": offs2, "wgt": wgt, "offs3": offs3,
            "w3": w3, "w4_words": w4_words, "w4_scales": w4_scales}

def reference(tab_words, tab_scales, offs, w1, w2_words, w2_scales, phase, gain,
              page0, wgs, offs2, wgt, offs3, w3, w4_words, w4_scales):
    v = unpack_weight(tab_words, tab_scales, "e4m3")[:, unstriped(offs)]
    w2 = unpack_weight(w2_words, w2_scales, "e4m3")
    w4 = unpack_weight(w4_words, w4_scales, "e2m1")
    a = mxq(f64(w1), 0, "e4m3").T @ v
    b = w2.T @ v
    h = f64(gain)[:, None] * np.exp(a) * np.sin(b + f64(phase)[:, None])
    page = f64(page0).copy()
    page[:, unstriped(offs2)] = np.tile(f64(wgs), (H // 128, 1)) * h
    x = heads(page, f64(wgt), unstriped8(offs3))
    xq = mxq(x, 0, "e4m3")
    y = mxq(f64(w3), 0, "e4m3").T @ xq + w4.T @ v
    return y

@@ -1,0 +1,263 @@
+import math
+from contextlib import ExitStack
+
+import concourse.mybir as mybir
+
+K, T, S, H, T2, N = 1024, 2048, 512, 1024, 1024, 512
+FLOPS = 2 * K * H * S * 2 + 2 * H * N * S + 2 * K * N * S
+
+F32 = mybir.dt.float32
+BF16 = mybir.dt.bfloat16
+I32 = mybir.dt.int32
+U32 = mybir.dt.uint32
+U16 = mybir.dt.uint16
+U8 = mybir.dt.uint8
+E4M3 = mybir.dt.float8_e4m3fn_x4
+E2M1 = mybir.dt.float4_e2m1fn_x4
+ACT = mybir.ActivationFunctionType
+ALU = mybir.AluOpType
+
+P = 128
+PACK = 4
+KP = P * PACK
+HALF = S // 2
+ROUNDER = 1.5 * 2.0**23
+
+
+def tile_list_interference_lane_scores_kernel(
+    tc, tab_words, tab_scales, offs, w1, w2_words, w2_scales, phase, gain,
+    page0, wgs, offs2, wgt, offs3, w3, w4_words, w4_scales, out,
+):
+    nc = tc.nc
+    with ExitStack() as ctx:
+        keep = ctx.enter_context(tc.tile_pool(name="keep", bufs=1))
+        stage = ctx.enter_context(tc.tile_pool(name="stage", bufs=4))
+        rounded = ctx.enter_context(tc.tile_pool(name="rounded", bufs=3))
+        psum = ctx.enter_context(tc.psum_pool(name="psum", bufs=1))
+
+        def held(shape, dtype, name):
+            return keep.tile(shape, dtype, name=name, align_bytes=64)
+
+        picks = keep.tile([P, S // 16], U16, name="picks")
+        cells = keep.tile([P, S // 16], U16, name="cells")
+        lanes = keep.tile([P, S // 16], U16, name="lanes")
+
+        tab_w = [held([P, T], U32, f"tab_w{a}") for a in range(2)]
+        tab_s = held([P, T], U8, "tab_s")
+        v_w = [held([P, S], U32, f"v_w{a}") for a in range(2)]
+        v_s = held([P, S], U8, "v_s")
+        v_s1 = held([P, S], U8, "v_s1")
+        w2_s_raw = held([P, H], U8, "w2_s_raw")
+        w2_s = held([P, H], U8, "w2_s")
+        w2_w = [held([P, 2, KP], U32, f"w2_w{b}") for b in range(2)]
+        w1_w = [[held([P, KP], U32, f"w1_w{b}{a}") for a in range(2)] for b in range(2)]
+        w1_s = [[held([P, KP], U8, f"w1_s{b}{a}") for a in range(2)] for b in range(2)]
+        w3_w = [held([P, N], U32, f"w3_w{b}") for b in range(2)]
+        w3_s = [held([P, N], U8, f"w3_s{b}") for b in range(2)]
+        w4_w = held([P, 2, 2 * N], U8, "w4_w")
+        w4_s = held([P, 2, N], U8, "w4_s")
+        phase_sb = held([P, 2, PACK], F32, "phase_sb")
+        phase_turns = held([P, 2, PACK], F32, "phase_turns")
+        gain_sb = held([P, 2, PACK], F32, "gain_sb")
+        wgs_sb = held([P, PACK * S], F32, "wgs_sb")
+        wgt_sb = held([P, S], F32, "wgt_sb")
+        page = [[held([P, T2], F32, f"page{b}{i}") for i in range(PACK)] for b in range(2)]
+
+        nc.vector.memset(tab_s[:].bitcast(I32), 0)
+        nc.vector.memset(w2_s_raw[:].bitcast(I32), 0)
+        nc.gpsimd.memset(w4_s[:].rearrange("p a n -> p (a n)").bitcast(I32), 0)
+        nc.gpsimd.memset(v_s1[:].bitcast(I32), 0)
+
+        def load_tab_words(a):
+            nc.sync.dma_start(out=tab_w[a][:].bitcast(I32),
+                              in_=tab_words[a].rearrange("p t i -> p (t i)").bitcast(I32))
+
+        def load_packed_scales(tile, scales, q):
+            nc.sync.dma_start(out=tile[32 * q : 32 * q + 8, :].bitcast(I32),
+                              in_=scales[:, 4 * q : 4 * q + 4, :].bitcast(I32))
+
+        def load_w2_words(b):
+            raw = keep.tile([P, 2, KP], U32, name="w2_raw", tag="w2_raw", align_bytes=64)
+            src = w2_words.rearrange("a p c i -> p a (c i)")[:, :, PACK * KP * b : PACK * KP * (b + 1)]
+            nc.sync.dma_start(out=raw[:].bitcast(I32), in_=src.bitcast(I32))
+            return raw
+
+        def load_rows(w, a, cols):
+            raw = stage.tile([P, PACK, KP], F32, name="raw", tag="raw")
+            nc.sync.dma_start(out=raw[:], in_=w[KP * a : KP * (a + 1), cols].rearrange("(p j) c -> p j c", j=PACK))
+            return raw
+
+        page_rows = page0.rearrange("(b p i) c -> b i p c", b=2, i=PACK)
+
+        def load_page(b, i):
+            nc.sync.dma_start(out=page[b][i][:], in_=page_rows[b, i])
+
+        def deal_w2(b, raw):
+            nc.vector.tensor_copy(
+                out=w2_w[b][:].bitcast(I32).rearrange("p a (t g m) -> p a g t m", t=PACK, m=4),
+                in_=raw[:].bitcast(I32).rearrange("p a (g m t) -> p a g t m", t=PACK, m=4))
+
+        def copy_on(engine, out, in_):
+            if engine == "vector":
+                nc.vector.tensor_copy(out=out, in_=in_)
+            else:
+                nc.scalar.copy(out=out, in_=in_)
+
+        def quantize(codes, scales, grouped):
+            nc.vector.quantize_mx(out=codes.bitcast(E4M3), scales=scales, in_=grouped)
+
+        def round_w1(engine, raw):
+            grouped = rounded.tile([P, PACK * KP], BF16, name="grouped", tag="grouped", align_bytes=64)
+            copy_on(engine, grouped[:].rearrange("p (t m j) -> p m t j", t=PACK, j=PACK),
+                    raw[:].rearrange("p j (m t) -> p m t j", t=PACK))
+            return grouped
+
+        def round_rows(engine, raw, width):
+            grouped = rounded.tile([P, PACK * width], BF16, name="grouped", tag="grouped", align_bytes=64)
+            copy_on(engine, grouped[:].rearrange("p (c i t) -> p c t i", i=4, t=PACK),
+                    raw.rearrange("p t (c i) -> p c t i", i=4))
+            return grouped
+
+        def first_product(kind, lhs_w, lhs_s):
+            acc = psum.tile([P, S], F32, name=kind, tag=kind, bufs=2)
+            for a in range(2):
+                nc.tensor.matmul_mx(out=acc[:], lhsT=lhs_w(a).bitcast(E4M3), lhsT_scale=lhs_s(a),
+                                    rhs=v_w[a][:].bitcast(E4M3), rhs_scale=v_s[4 * a :, :],
+                                    start=(a == 0), stop=(a == 1))
+            return acc
+
+        def sines(b):
+            turns = keep.tile([P, PACK * S], F32, name="turns", tag="turns")
+            whole = keep.tile([P, PACK * S], U32, name="whole", tag="whole")
+            rest = keep.tile([P, PACK * S], F32, name=f"rest{b}")
+            sine = keep.tile([P, PACK * S], F32, name=f"sine{b}")
+            factor = keep.tile([P, PACK * S], F32, name=f"factor{b}")
+            for pair in range(2):
+                both = slice(2 * S * pair, 2 * S * (pair + 1))
+                for i in (2 * pair, 2 * pair + 1):
+                    cols = slice(P * i, P * (i + 1))
+                    acc = first_product("phase_sum", lambda a: w2_w[b][:, a, cols],
+                                        lambda a: w2_s[4 * a :, KP * b + P * i : KP * b + P * (i + 1)])
+                    nc.scalar.activation(out=turns[:, S * i : S * (i + 1)], in_=acc[:], func=ACT.Identity,
+                                         scale=1.0 / (2.0 * math.pi), bias=phase_turns[:, b, i : i + 1])
+                nc.scalar.activation(out=whole[:, both], in_=turns[:, both], func=ACT.Copy, bias=ROUNDER)
+                nc.vector.scalar_tensor_tensor(out=rest[:, both], in0=whole[:, both].bitcast(I32), scalar=ROUNDER,
+                                               in1=turns[:, both], op0=ALU.subtract, op1=ALU.subtract)
+                nc.scalar.activation(out=sine[:, both], in_=rest[:, both], func=ACT.Sin, scale=-2.0 * math.pi)
+                for i in (2 * pair, 2 * pair + 1):
+                    own = slice(S * i, S * (i + 1))
+                    nc.vector.scalar_tensor_tensor(out=factor[:, own], in0=sine[:, own], scalar=gain_sb[:, b, i : i + 1],
+                                                   in1=wgs_sb[:, own], op0=ALU.mult, op1=ALU.mult)
+            homes = [rest[:, 2 * S : 3 * S], rest[:, 3 * S :], sine[:, 2 * S : 3 * S], sine[:, 3 * S :]]
+            return factor, homes
+
+        def replace_cells(b, factor, homes):
+            for i in range(PACK):
+                cols = slice(P * i, P * (i + 1))
+                acc = first_product("log_amp", lambda a: w1_w[b][a][:, cols], lambda a: w1_s[b][a][:, cols])
+                nc.scalar.activation(out=homes[i], in_=acc[:], func=ACT.Exp)
+                nc.vector.tensor_tensor(page[b][i][:].indirect(cells[:]), homes[i], factor[:, S * i : S * (i + 1)], ALU.mult)
+
+        def gather_x(b, first, width):
+            picked = keep.tile([P, PACK, width], F32, name="picked", tag=f"picked{first}")
+            for i in range(PACK):
+                nc.vector.tensor_tensor(picked[:, i, :], page[b][i][:].indirect(lanes[:, first // 16 : (first + width) // 16]),
+                                        wgt_sb[:, first : first + width], ALU.mult)
+            return picked
+
+        nc.sync.dma_start(picks[:], offs)
+        load_tab_words(0)
+        for q in range(4):
+            load_packed_scales(tab_s, tab_scales, q)
+        load_tab_words(1)
+        nc.sync.dma_start(out=phase_sb[:], in_=phase.rearrange("(b p i) -> p b i", b=2, i=PACK))
+        for q in range(4):
+            load_packed_scales(w2_s_raw, w2_scales, q)
+        w2_raw = load_w2_words(0)
+        w1_raw = [load_rows(w1, a, slice(0, KP)) for a in range(2)]
+        nc.sync.dma_start(out=gain_sb[:], in_=gain.rearrange("(b p i) -> p b i", b=2, i=PACK))
+        for q in range(4):
+            nc.sync.dma_start(out=wgs_sb[32 * q : 32 * (q + 1), :], in_=wgs.rearrange("(m i) j -> m (i j)", i=PACK))
+        nc.sync.dma_start(cells[:], offs2)
+        load_page(0, 0)
+
+        nc.vector.tensor_copy(v_w[0][:], tab_w[0][:].indirect(picks[:]))
+        nc.vector.tensor_copy(v_s[:], tab_s[:].indirect(picks[:]))
+        nc.vector.tensor_copy(v_w[1][:], tab_w[1][:].indirect(picks[:]))
+        nc.vector.tensor_copy(out=w2_s[:].rearrange("p (b t m) -> p b t m", b=2, t=PACK),
+                              in_=w2_s_raw[:].rearrange("p (b m t) -> p b t m", b=2, t=PACK))
+        deal_w2(0, w2_raw)
+        nc.scalar.activation(out=phase_turns[:], in_=phase_sb[:], func=ACT.Copy, scale=1.0 / (2.0 * math.pi))
+        for a in range(2):
+            quantize(w1_w[0][a][:], w1_s[0][a][:], round_w1("vector", w1_raw[a])[:])
+        factor, homes = sines(0)
+        replace_cells_first = (factor, homes)
+
+        w2_raw = load_w2_words(1)
+        load_page(0, 1)
+        w1_raw = [load_rows(w1, 0, slice(KP, H))]
+        load_page(0, 2)
+        w1_raw.append(load_rows(w1, 1, slice(KP, H)))
+        load_page(0, 3)
+        for q in range(4):
+            nc.sync.dma_start(out=v_s1[32 * q : 32 * q + 4, :].bitcast(I32), in_=v_s[32 * q + 4 : 32 * q + 8, :].bitcast(I32))
+        w3_raw = [load_rows(w3, 0, slice(0, N))]
+        nc.sync.dma_start(lanes[:], offs3)
+        nc.sync.dma_start(out=wgt_sb[:], in_=wgt)
+        load_page(1, 0)
+        load_page(1, 1)
+        w3_raw.append(load_rows(w3, 1, slice(0, N)))
+        load_page(1, 2)
+        nc.sync.dma_start(out=w4_w[:].bitcast(I32), in_=w4_words.rearrange("a p c -> p a c").bitcast(I32))
+        for q in range(4):
+            nc.sync.dma_start(out=w4_s[32 * q : 32 * q + 4].bitcast(I32),
+                              in_=w4_scales[:, 4 * q : 4 * q + 4, :].rearrange("a q n -> q a n").bitcast(I32))
+        load_page(1, 3)
+
+        replace_cells(0, *replace_cells_first)
+        deal_w2(1, w2_raw)
+        factor, homes = sines(1)
+        for a in range(2):
+            quantize(w1_w[1][a][:], w1_s[1][a][:], round_w1("scalar", w1_raw[a])[:])
+        picked0 = [gather_x(0, HALF * h, HALF) for h in range(2)]
+        replace_cells(1, factor, homes)
+        x_w = [[held([P, HALF], U32, f"x_w{b}{h}") for h in range(2)] for b in range(2)]
+        x_s = [[held([P, HALF], U8, f"x_s{b}{h}") for h in range(2)] for b in range(2)]
+        for b in range(2):
+            quantize(w3_w[b][:], w3_s[b][:], round_rows("scalar", w3_raw[b][:], N)[:])
+        for h in range(2):
+            quantize(x_w[0][h][:], x_s[0][h][:], round_rows("scalar", picked0[h][:], HALF)[:])
+
+        scores = [[psum.tile([P, 2, HALF], F32, name=f"scores{h}{m}") for m in range(2)] for h in range(2)]
+        v_planes = [v_s, v_s1]
+        for h in range(2):
+            lane_cols = slice(HALF * h, HALF * (h + 1))
+            for m in range(2):
+                for u in range(2):
+                    n0 = P * (2 * m + u)
+                    for a in range(2):
+                        nc.tensor.matmul_mx(out=scores[h][m][:, u, :],
+                                            lhsT=w4_w[:, a, 2 * n0 : 2 * (n0 + P)].bitcast(E2M1), lhsT_scale=w4_s[:, a, n0 : n0 + P],
+                                            rhs=v_w[a][:, lane_cols].bitcast(E4M3), rhs_scale=v_planes[a][:, lane_cols],
+                                            start=(u == 0 and a == 0), stop=False)
+
+        def score_pass(b, h):
+            for m in range(2):
+                for u in range(2):
+                    n0 = P * (2 * m + u)
+                    nc.tensor.matmul_mx(out=scores[h][m][:, u, :],
+                                        lhsT=w3_w[b][:, n0 : n0 + P].bitcast(E4M3), lhsT_scale=w3_s[b][:, n0 : n0 + P],
+                                        rhs=x_w[b][h][:].bitcast(E4M3), rhs_scale=x_s[b][h][:],
+                                        start=False, stop=(b == 1 and u == 1))
+
+        for h in range(2):
+            score_pass(0, h)
+        out_rows = out.rearrange("(m u p) j -> m p u j", m=2, u=2)
+        for h in range(2):
+            picked = gather_x(1, HALF * h, HALF)
+            quantize(x_w[1][h][:], x_s[1][h][:], round_rows("scalar" if h == 0 else "vector", picked[:], HALF)[:])
+            score_pass(1, h)
+            for m in range(2):
+                result = keep.tile([P, 2, HALF], F32, name=f"result{h}{m}")
+                copy_on("scalar" if (h == 0 or m == 0) else "vector", result[:], scores[h][m][:])
+                nc.sync.dma_start(out=out_rows[m][:, :, HALF * h : HALF * (h + 1)], in_=result[:])

@@ -2,6 +2,7 @@ import math
 from contextlib import ExitStack
 
 import concourse.mybir as mybir
+from concourse.masks import make_identity
 
 K, T, S, H, T2, N = 1024, 2048, 512, 1024, 1024, 512
 FLOPS = 2 * K * H * S * 2 + 2 * H * N * S + 2 * K * N * S
@@ -106,65 +107,93 @@ def tile_list_interference_lane_scores_kernel(
         def quantize(codes, scales, grouped):
             nc.vector.quantize_mx(out=codes.bitcast(E4M3), scales=scales, in_=grouped)
 
-        def round_w1(engine, raw):
-            grouped = rounded.tile([P, PACK * KP], BF16, name="grouped", tag="grouped", align_bytes=64)
-            copy_on(engine, grouped[:].rearrange("p (t m j) -> p m t j", t=PACK, j=PACK),
-                    raw[:].rearrange("p j (m t) -> p m t j", t=PACK))
+        def grouped_tile(width, tag):
+            if tag is None:
+                return rounded.tile([P, PACK * width], BF16, name="grouped", tag="grouped", align_bytes=64)
+            return keep.tile([P, PACK * width], BF16, name="grouped", tag=tag, align_bytes=64)
+
+        def round_w1(engines, raw, tag=None):
+            grouped = grouped_tile(KP, tag)
+            share = P // len(engines)
+            for n, engine in enumerate(engines):
+                copy_on(engine, grouped[:].rearrange("p (t m j) -> p m t j", t=PACK, j=PACK)[:, share * n : share * (n + 1)],
+                        raw[:].rearrange("p j (m t) -> p m t j", t=PACK)[:, share * n : share * (n + 1)])
             return grouped
 
-        def round_rows(engine, raw, width):
-            grouped = rounded.tile([P, PACK * width], BF16, name="grouped", tag="grouped", align_bytes=64)
+        def round_rows(engine, raw, width, tag=None):
+            grouped = grouped_tile(width, tag)
             copy_on(engine, grouped[:].rearrange("p (c i t) -> p c t i", i=4, t=PACK),
                     raw.rearrange("p t (c i) -> p c t i", i=4))
             return grouped
 
-        def first_product(kind, lhs_w, lhs_s):
-            acc = psum.tile([P, S], F32, name=kind, tag=kind, bufs=2)
+        banks = [psum.tile([P, S], F32, name=f"bank{n}") for n in range(8)]
+
+        def first_product(bank, lhs_w, lhs_s):
+            acc = banks[bank]
             for a in range(2):
                 nc.tensor.matmul_mx(out=acc[:], lhsT=lhs_w(a).bitcast(E4M3), lhsT_scale=lhs_s(a),
                                     rhs=v_w[a][:].bitcast(E4M3), rhs_scale=v_s[4 * a :, :],
                                     start=(a == 0), stop=(a == 1))
             return acc
 
-        def sines(b):
-            turns = keep.tile([P, PACK * S], F32, name="turns", tag="turns")
-            whole = keep.tile([P, PACK * S], U32, name="whole", tag="whole")
-            rest = keep.tile([P, PACK * S], F32, name=f"rest{b}")
-            sine = keep.tile([P, PACK * S], F32, name=f"sine{b}")
-            factor = keep.tile([P, PACK * S], F32, name=f"factor{b}")
-            for pair in range(2):
-                both = slice(2 * S * pair, 2 * S * (pair + 1))
-                for i in (2 * pair, 2 * pair + 1):
-                    cols = slice(P * i, P * (i + 1))
-                    acc = first_product("phase_sum", lambda a: w2_w[b][:, a, cols],
-                                        lambda a: w2_s[4 * a :, KP * b + P * i : KP * b + P * (i + 1)])
-                    nc.scalar.activation(out=turns[:, S * i : S * (i + 1)], in_=acc[:], func=ACT.Identity,
-                                         scale=1.0 / (2.0 * math.pi), bias=phase_turns[:, b, i : i + 1])
-                nc.scalar.activation(out=whole[:, both], in_=turns[:, both], func=ACT.Copy, bias=ROUNDER)
-                nc.vector.scalar_tensor_tensor(out=rest[:, both], in0=whole[:, both].bitcast(I32), scalar=ROUNDER,
-                                               in1=turns[:, both], op0=ALU.subtract, op1=ALU.subtract)
-                nc.scalar.activation(out=sine[:, both], in_=rest[:, both], func=ACT.Sin, scale=-2.0 * math.pi)
-                for i in (2 * pair, 2 * pair + 1):
-                    own = slice(S * i, S * (i + 1))
-                    nc.vector.scalar_tensor_tensor(out=factor[:, own], in0=sine[:, own], scalar=gain_sb[:, b, i : i + 1],
-                                                   in1=wgs_sb[:, own], op0=ALU.mult, op1=ALU.mult)
-            homes = [rest[:, 2 * S : 3 * S], rest[:, 3 * S :], sine[:, 2 * S : 3 * S], sine[:, 3 * S :]]
-            return factor, homes
+        turns = [keep.tile([P, 2 * S], F32, name="turns", tag=f"turns{n}", align_bytes=64) for n in range(2)]
+        whole = keep.tile([P, PACK * S], U32, name="whole")
+        ring = [keep.tile([P, 2 * S], F32, name=f"ring{n}") for n in range(4)]
+        sine = [keep.tile([P, PACK * S], F32, name=f"sine{b}") for b in range(2)]
 
-        def replace_cells(b, factor, homes):
-            for i in range(PACK):
-                cols = slice(P * i, P * (i + 1))
-                acc = first_product("log_amp", lambda a: w1_w[b][a][:, cols], lambda a: w1_s[b][a][:, cols])
-                nc.scalar.activation(out=homes[i], in_=acc[:], func=ACT.Exp)
-                nc.vector.tensor_tensor(page[b][i][:].indirect(cells[:]), homes[i], factor[:, S * i : S * (i + 1)], ALU.mult)
+        def slot(tile_, i, count=1):
+            return tile_[:, S * i : S * (i + count)]
 
-        def gather_x(b, first, width):
-            picked = keep.tile([P, PACK, width], F32, name="picked", tag=f"picked{first}")
+        def phase_in_turns(b, i, bank):
+            cols = slice(P * i, P * (i + 1))
+            acc = first_product(bank, lambda a: w2_w[b][:, a, cols],
+                                lambda a: w2_s[4 * a :, KP * b + P * i : KP * b + P * (i + 1)])
+            nc.scalar.activation(out=slot(turns[i // 2], i % 2), in_=acc[:], func=ACT.Identity,
+                                 scale=1.0 / (2.0 * math.pi), bias=phase_turns[:, b, i : i + 1])
+
+        def drop_whole_turns(i, count, engine, home):
+            if engine == "vector":
+                nc.vector.tensor_scalar(out=slot(whole, i, count).bitcast(I32), in0=slot(turns[i // 2], i % 2, count),
+                                        scalar1=ROUNDER, scalar2=None, op0=ALU.add)
+            else:
+                nc.scalar.activation(out=slot(whole, i, count), in_=slot(turns[i // 2], i % 2, count), func=ACT.Copy, bias=ROUNDER)
+            nc.vector.scalar_tensor_tensor(out=home, in0=slot(whole, i, count).bitcast(I32), scalar=ROUNDER,
+                                           in1=slot(turns[i // 2], i % 2, count), op0=ALU.subtract, op1=ALU.subtract)
+            return home
+
+        def reduce_pair(b, pair, first_bank, home):
+            for i in (2 * pair, 2 * pair + 1):
+                phase_in_turns(b, i, first_bank + i % 2)
+            return drop_whole_turns(2 * pair, 2, "scalar", home)
+
+        def take_sine(b, i, count, rest):
+            nc.scalar.activation(out=slot(sine[b], i, count), in_=rest, func=ACT.Sin, scale=-2.0 * math.pi)
+
+        def make_factor(b, i, home):
+            nc.vector.scalar_tensor_tensor(out=home, in0=slot(sine[b], i), scalar=gain_sb[:, b, i : i + 1],
+                                           in1=slot(wgs_sb, i), op0=ALU.mult, op1=ALU.mult)
+            return home
+
+        def amplitude(b, i, bank, home):
+            cols = slice(P * i, P * (i + 1))
+            acc = first_product(bank, lambda a: w1_w[b][a][:, cols], lambda a: w1_s[b][a][:, cols])
+            nc.scalar.activation(out=home, in_=acc[:], func=ACT.Exp)
+            return home
+
+        def replace_cells(b, i, amp, factor):
+            nc.vector.tensor_tensor(page[b][i][:].indirect(cells[:]), amp, factor, ALU.mult)
+
+        def gather_x(b, first, width, tag):
+            picked = keep.tile([P, PACK, width], F32, name="picked", tag=tag, align_bytes=64)
             for i in range(PACK):
                 nc.vector.tensor_tensor(picked[:, i, :], page[b][i][:].indirect(lanes[:, first // 16 : (first + width) // 16]),
                                         wgt_sb[:, first : first + width], ALU.mult)
             return picked
 
+        identity = held([P, P], F32, "identity")
+        make_identity(nc, identity[:])
+        wgs_raw = held([P, S], F32, "wgs_raw")
+        nc.sync.dma_start(out=wgs_raw[:], in_=wgs)
         nc.sync.dma_start(picks[:], offs)
         load_tab_words(0)
         for q in range(4):
@@ -176,10 +205,19 @@ def tile_list_interference_lane_scores_kernel(
         w2_raw = load_w2_words(0)
         w1_raw = [load_rows(w1, a, slice(0, KP)) for a in range(2)]
         nc.sync.dma_start(out=gain_sb[:], in_=gain.rearrange("(b p i) -> p b i", b=2, i=PACK))
-        for q in range(4):
-            nc.sync.dma_start(out=wgs_sb[32 * q : 32 * (q + 1), :], in_=wgs.rearrange("(m i) j -> m (i j)", i=PACK))
         nc.sync.dma_start(cells[:], offs2)
         load_page(0, 0)
+
+        for c in range(4):
+            nc.tensor.transpose(banks[7][:, P * c : P * (c + 1)], wgs_raw[:, P * c : P * (c + 1)], identity[:])
+        wgs_turned = held([P, PACK, S], F32, "wgs_turned")
+        by_slot = banks[7][:].rearrange("p (c m i) -> p i c m", c=4, i=PACK)
+        for i, bank in enumerate([0, 1, 4, 5]):
+            nc.scalar.copy(out=wgs_turned[:, i, :].rearrange("p (c q m) -> p c q m", c=4, q=4),
+                           in_=by_slot[:, i].unsqueeze(2).broadcast_to([P, 4, 4, 32]))
+            for c in range(4):
+                nc.tensor.transpose(banks[bank][:, P * c : P * (c + 1)], wgs_turned[:, i, P * c : P * (c + 1)], identity[:])
+            nc.scalar.copy(out=slot(wgs_sb, i), in_=banks[bank][:])
 
         nc.vector.tensor_copy(v_w[0][:], tab_w[0][:].indirect(picks[:]))
         nc.vector.tensor_copy(v_s[:], tab_s[:].indirect(picks[:]))
@@ -188,76 +226,97 @@ def tile_list_interference_lane_scores_kernel(
                               in_=w2_s_raw[:].rearrange("p (b m t) -> p b t m", b=2, t=PACK))
         deal_w2(0, w2_raw)
         nc.scalar.activation(out=phase_turns[:], in_=phase_sb[:], func=ACT.Copy, scale=1.0 / (2.0 * math.pi))
-        for a in range(2):
-            quantize(w1_w[0][a][:], w1_s[0][a][:], round_w1("vector", w1_raw[a])[:])
-        factor, homes = sines(0)
-        replace_cells_first = (factor, homes)
+        for i in range(2):
+            phase_in_turns(0, i, 2 + i)
+            take_sine(0, i, 1, drop_whole_turns(i, 1, "vector", slot(ring[i], 0)))
+        for a, engines in enumerate([["vector"], ["scalar", "vector"]]):
+            quantize(w1_w[0][a][:], w1_s[0][a][:], round_w1(engines, w1_raw[a], [None, "turns0"][a])[:])
+        first_home = keep.tile([P, S], F32, name="first_home")
+        factor = [make_factor(0, 0, first_home[:]), make_factor(0, 1, slot(ring[1], 1))]
 
         w2_raw = load_w2_words(1)
-        load_page(0, 1)
-        w1_raw = [load_rows(w1, 0, slice(KP, H))]
-        load_page(0, 2)
-        w1_raw.append(load_rows(w1, 1, slice(KP, H)))
-        load_page(0, 3)
-        for q in range(4):
-            nc.sync.dma_start(out=v_s1[32 * q : 32 * q + 4, :].bitcast(I32), in_=v_s[32 * q + 4 : 32 * q + 8, :].bitcast(I32))
-        w3_raw = [load_rows(w3, 0, slice(0, N))]
+        for i in range(1, PACK):
+            load_page(0, i)
+        w1_raw = [load_rows(w1, a, slice(KP, H)) for a in range(2)]
         nc.sync.dma_start(lanes[:], offs3)
         nc.sync.dma_start(out=wgt_sb[:], in_=wgt)
-        load_page(1, 0)
-        load_page(1, 1)
-        w3_raw.append(load_rows(w3, 1, slice(0, N)))
-        load_page(1, 2)
         nc.sync.dma_start(out=w4_w[:].bitcast(I32), in_=w4_words.rearrange("a p c -> p a c").bitcast(I32))
         for q in range(4):
             nc.sync.dma_start(out=w4_s[32 * q : 32 * q + 4].bitcast(I32),
                               in_=w4_scales[:, 4 * q : 4 * q + 4, :].rearrange("a q n -> q a n").bitcast(I32))
-        load_page(1, 3)
+        for q in range(4):
+            nc.sync.dma_start(out=v_s1[32 * q : 32 * q + 4, :].bitcast(I32), in_=v_s[32 * q + 4 : 32 * q + 8, :].bitcast(I32))
+        for i in range(PACK):
+            load_page(1, i)
+        w3_raw = [load_rows(w3, b, slice(0, N)) for b in range(2)]
 
-        replace_cells(0, *replace_cells_first)
+        amp_homes = [slot(ring[1], 0), slot(ring[0], 1), slot(ring[2], 0), slot(ring[3], 0)]
+        amp = [amplitude(0, i, i, amp_homes[i]) for i in range(PACK)]
+        replace_cells(0, 0, amp[0], factor[0])
         deal_w2(1, w2_raw)
-        factor, homes = sines(1)
+        replace_cells(0, 1, amp[1], factor[1])
+        take_sine(0, 2, 2, reduce_pair(0, 1, 0, ring[0][:]))
+        turns = [keep.tile([P, 2 * S], F32, name="turns", tag="turns0", align_bytes=64), turns[1]]
+        take_sine(1, 0, 2, reduce_pair(1, 0, 4, ring[1][:]))
+        factor = [make_factor(0, i, slot(ring[i], 1)) for i in (2, 3)]
+        replace_cells(0, 2, amp[2], factor[0])
+        take_sine(1, 2, 2, reduce_pair(1, 1, 6, ring[2][:]))
+        replace_cells(0, 3, amp[3], factor[1])
+        factor = [make_factor(1, i, slot(ring[3 - 3 * (i // 2)], i % 2)) for i in range(PACK)]
         for a in range(2):
-            quantize(w1_w[1][a][:], w1_s[1][a][:], round_w1("scalar", w1_raw[a])[:])
-        picked0 = [gather_x(0, HALF * h, HALF) for h in range(2)]
-        replace_cells(1, factor, homes)
-        x_w = [[held([P, HALF], U32, f"x_w{b}{h}") for h in range(2)] for b in range(2)]
-        x_s = [[held([P, HALF], U8, f"x_s{b}{h}") for h in range(2)] for b in range(2)]
-        for b in range(2):
-            quantize(w3_w[b][:], w3_s[b][:], round_rows("scalar", w3_raw[b][:], N)[:])
-        for h in range(2):
-            quantize(x_w[0][h][:], x_s[0][h][:], round_rows("scalar", picked0[h][:], HALF)[:])
+            quantize(w1_w[1][a][:], w1_s[1][a][:], round_w1(["scalar"], w1_raw[a], f"late{a}")[:])
+        picked0 = [gather_x(0, HALF * h, HALF, f"late{h}") for h in range(2)]
+        amp = [amplitude(1, i, i % 2, slot(ring[2 - i // 2], i % 2)) for i in range(PACK)]
+        for i in range(PACK):
+            replace_cells(1, i, amp[i], factor[i])
+        x_w = [held([P, S], U32, f"x_w{b}") for b in range(2)]
+        x_s = [held([P, S], U8, f"x_s{b}") for b in range(2)]
 
-        scores = [[psum.tile([P, 2, HALF], F32, name=f"scores{h}{m}") for m in range(2)] for h in range(2)]
+        def quantize_x(b, first, width, engine, picked, tag=None):
+            lane_cols = slice(first, first + width)
+            quantize(x_w[b][:, lane_cols], x_s[b][:, lane_cols], round_rows(engine, picked[:], width, tag)[:])
+
+        quantize_x(0, 0, HALF, "scalar", picked0[0])
+        quantize_x(0, HALF, HALF, "scalar", picked0[1])
+        for b, tag in enumerate([None, "late0"]):
+            quantize(w3_w[b][:], w3_s[b][:], round_rows("scalar", w3_raw[b][:], N, tag)[:])
+
+        scores = [banks[4 + c][:].rearrange("p (m j) -> p m j", m=4) for c in range(4)]
         v_planes = [v_s, v_s1]
-        for h in range(2):
-            lane_cols = slice(HALF * h, HALF * (h + 1))
-            for m in range(2):
-                for u in range(2):
-                    n0 = P * (2 * m + u)
-                    for a in range(2):
-                        nc.tensor.matmul_mx(out=scores[h][m][:, u, :],
-                                            lhsT=w4_w[:, a, 2 * n0 : 2 * (n0 + P)].bitcast(E2M1), lhsT_scale=w4_s[:, a, n0 : n0 + P],
-                                            rhs=v_w[a][:, lane_cols].bitcast(E4M3), rhs_scale=v_planes[a][:, lane_cols],
-                                            start=(u == 0 and a == 0), stop=False)
+        def score_pass(b, c):
+            lane_cols = slice(P * c, P * (c + 1))
+            for m in range(4):
+                nc.tensor.matmul_mx(out=scores[c][:, m, :],
+                                    lhsT=w3_w[b][:, P * m : P * (m + 1)].bitcast(E4M3), lhsT_scale=w3_s[b][:, P * m : P * (m + 1)],
+                                    rhs=x_w[b][:, lane_cols].bitcast(E4M3), rhs_scale=x_s[b][:, lane_cols],
+                                    start=False, stop=(b == 1 and m == 3))
 
-        def score_pass(b, h):
-            for m in range(2):
-                for u in range(2):
-                    n0 = P * (2 * m + u)
-                    nc.tensor.matmul_mx(out=scores[h][m][:, u, :],
-                                        lhsT=w3_w[b][:, n0 : n0 + P].bitcast(E4M3), lhsT_scale=w3_s[b][:, n0 : n0 + P],
-                                        rhs=x_w[b][h][:].bitcast(E4M3), rhs_scale=x_s[b][h][:],
-                                        start=False, stop=(b == 1 and u == 1))
+        for c in range(4):
+            lane_cols = slice(P * c, P * (c + 1))
+            for m in range(4):
+                for a in range(2):
+                    nc.tensor.matmul_mx(out=scores[c][:, m, :],
+                                        lhsT=w4_w[:, a, 2 * P * m : 2 * P * (m + 1)].bitcast(E2M1), lhsT_scale=w4_s[:, a, P * m : P * (m + 1)],
+                                        rhs=v_w[a][:, lane_cols].bitcast(E4M3), rhs_scale=v_planes[a][:, lane_cols],
+                                        start=(m == 0 and a == 0), stop=False)
 
-        for h in range(2):
-            score_pass(0, h)
-        out_rows = out.rearrange("(m u p) j -> m p u j", m=2, u=2)
-        for h in range(2):
-            picked = gather_x(1, HALF * h, HALF)
-            quantize(x_w[1][h][:], x_s[1][h][:], round_rows("scalar" if h == 0 else "vector", picked[:], HALF)[:])
-            score_pass(1, h)
-            for m in range(2):
-                result = keep.tile([P, 2, HALF], F32, name=f"result{h}{m}")
-                copy_on("scalar" if (h == 0 or m == 0) else "vector", result[:], scores[h][m][:])
-                nc.sync.dma_start(out=out_rows[m][:, :, HALF * h : HALF * (h + 1)], in_=result[:])
+        for c in range(4):
+            score_pass(0, c)
+        out_rows = out.rearrange("(m p) j -> p m j", m=4)
+
+        def finish(c, engine):
+            score_pass(1, c)
+            result = keep.tile([P, 4, P], F32, name=f"result{c}")
+            copy_on(engine, result[:], scores[c])
+            nc.sync.dma_start(out=out_rows[:, :, P * c : P * (c + 1)], in_=result[:])
+
+        picked = gather_x(1, 0, HALF, "late0")
+        third = gather_x(1, HALF, P, "late1")
+        quantize_x(1, 0, HALF, "scalar", picked, "tail")
+        finish(0, "scalar")
+        finish(1, "scalar")
+        fourth = gather_x(1, HALF + P, P, "tail")
+        quantize_x(1, HALF, P, "scalar", third)
+        finish(2, "scalar")
+        quantize_x(1, HALF + P, P, "vector", fourth)
+        finish(3, "vector")

@@ -73,12 +73,12 @@ def tile_list_interference_lane_scores_kernel(
             nc.sync.dma_start(out=tab_w[a][:].bitcast(I32),
                               in_=tab_words[a].rearrange("p t i -> p (t i)").bitcast(I32))
 
-        def load_packed_scales(tile, scales, q):
-            nc.sync.dma_start(out=tile[32 * q : 32 * q + 8, :].bitcast(I32),
+        def load_packed_scales(queue, tile, scales, q):
+            queue.dma_start(out=tile[32 * q : 32 * q + 8, :].bitcast(I32),
                               in_=scales[:, 4 * q : 4 * q + 4, :].bitcast(I32))
 
         def load_w2_words(b):
-            raw = keep.tile([P, 2, KP], U32, name="w2_raw", tag="w2_raw", align_bytes=64)
+            raw = keep.tile([P, 2, KP], U32, name=f"w2_raw{b}", align_bytes=64)
             src = w2_words.rearrange("a p c i -> p a (c i)")[:, :, PACK * KP * b : PACK * KP * (b + 1)]
             nc.sync.dma_start(out=raw[:].bitcast(I32), in_=src.bitcast(I32))
             return raw
@@ -114,10 +114,11 @@ def tile_list_interference_lane_scores_kernel(
 
         def round_w1(engines, raw, tag=None):
             grouped = grouped_tile(KP, tag)
-            share = P // len(engines)
-            for n, engine in enumerate(engines):
-                copy_on(engine, grouped[:].rearrange("p (t m j) -> p m t j", t=PACK, j=PACK)[:, share * n : share * (n + 1)],
-                        raw[:].rearrange("p j (m t) -> p m t j", t=PACK)[:, share * n : share * (n + 1)])
+            first = 0
+            for engine, share in engines:
+                copy_on(engine, grouped[:].rearrange("p (t m j) -> p m j t", t=PACK, j=PACK)[:, first : first + share],
+                        raw[:].rearrange("p j (m t) -> p m j t", t=PACK)[:, first : first + share])
+                first = first + share
             return grouped
 
         def round_rows(engine, raw, width, tag=None):
@@ -197,16 +198,14 @@ def tile_list_interference_lane_scores_kernel(
         nc.sync.dma_start(picks[:], offs)
         load_tab_words(0)
         for q in range(4):
-            load_packed_scales(tab_s, tab_scales, q)
+            load_packed_scales(nc.sync, tab_s, tab_scales, q)
         load_tab_words(1)
-        nc.sync.dma_start(out=phase_sb[:], in_=phase.rearrange("(b p i) -> p b i", b=2, i=PACK))
+        nc.scalar.dma_start(out=phase_sb[:], in_=phase.rearrange("(b p i) -> p b i", b=2, i=PACK))
         for q in range(4):
-            load_packed_scales(w2_s_raw, w2_scales, q)
+            load_packed_scales(nc.sync, w2_s_raw, w2_scales, q)
         w2_raw = load_w2_words(0)
         w1_raw = [load_rows(w1, a, slice(0, KP)) for a in range(2)]
-        nc.sync.dma_start(out=gain_sb[:], in_=gain.rearrange("(b p i) -> p b i", b=2, i=PACK))
-        nc.sync.dma_start(cells[:], offs2)
-        load_page(0, 0)
+        nc.scalar.dma_start(out=gain_sb[:], in_=gain.rearrange("(b p i) -> p b i", b=2, i=PACK))
 
         for c in range(4):
             nc.tensor.transpose(banks[7][:, P * c : P * (c + 1)], wgs_raw[:, P * c : P * (c + 1)], identity[:])
@@ -225,16 +224,18 @@ def tile_list_interference_lane_scores_kernel(
         nc.vector.tensor_copy(out=w2_s[:].rearrange("p (b t m) -> p b t m", b=2, t=PACK),
                               in_=w2_s_raw[:].rearrange("p (b m t) -> p b t m", b=2, t=PACK))
         deal_w2(0, w2_raw)
+        nc.sync.dma_start(cells[:], offs2)
+        load_page(0, 0)
+        w2_raw = load_w2_words(1)
         nc.scalar.activation(out=phase_turns[:], in_=phase_sb[:], func=ACT.Copy, scale=1.0 / (2.0 * math.pi))
         for i in range(2):
             phase_in_turns(0, i, 2 + i)
             take_sine(0, i, 1, drop_whole_turns(i, 1, "vector", slot(ring[i], 0)))
-        for a, engines in enumerate([["vector"], ["scalar", "vector"]]):
+        for a, engines in enumerate([[("vector", P)], [("scalar", 48), ("vector", 80)]]):
             quantize(w1_w[0][a][:], w1_s[0][a][:], round_w1(engines, w1_raw[a], [None, "turns0"][a])[:])
         first_home = keep.tile([P, S], F32, name="first_home")
         factor = [make_factor(0, 0, first_home[:]), make_factor(0, 1, slot(ring[1], 1))]
 
-        w2_raw = load_w2_words(1)
         for i in range(1, PACK):
             load_page(0, i)
         w1_raw = [load_rows(w1, a, slice(KP, H)) for a in range(2)]
@@ -264,7 +265,7 @@ def tile_list_interference_lane_scores_kernel(
         replace_cells(0, 3, amp[3], factor[1])
         factor = [make_factor(1, i, slot(ring[3 - 3 * (i // 2)], i % 2)) for i in range(PACK)]
         for a in range(2):
-            quantize(w1_w[1][a][:], w1_s[1][a][:], round_w1(["scalar"], w1_raw[a], f"late{a}")[:])
+            quantize(w1_w[1][a][:], w1_s[1][a][:], round_w1([("scalar", P)], w1_raw[a], f"late{a}")[:])
         picked0 = [gather_x(0, HALF * h, HALF, f"late{h}") for h in range(2)]
         amp = [amplitude(1, i, i % 2, slot(ring[2 - i // 2], i % 2)) for i in range(PACK)]
         for i in range(PACK):
@@ -281,42 +282,49 @@ def tile_list_interference_lane_scores_kernel(
         for b, tag in enumerate([None, "late0"]):
             quantize(w3_w[b][:], w3_s[b][:], round_rows("scalar", w3_raw[b][:], N, tag)[:])
 
-        scores = [banks[4 + c][:].rearrange("p (m j) -> p m j", m=4) for c in range(4)]
+        homes = [[(4, 4)], [(5, 4)], [(6, 4)], [(7, 2), (3, 2)]]
+        scores = [[banks[bank][:, P * m : P * (m + 1)] for bank, count in homes[c] for m in range(count)] for c in range(4)]
+        opens = [[m == 0 for bank, count in homes[c] for m in range(count)] for c in range(4)]
+        closes = [[m == count - 1 for bank, count in homes[c] for m in range(count)] for c in range(4)]
         v_planes = [v_s, v_s1]
         def score_pass(b, c):
             lane_cols = slice(P * c, P * (c + 1))
             for m in range(4):
-                nc.tensor.matmul_mx(out=scores[c][:, m, :],
+                nc.tensor.matmul_mx(out=scores[c][m],
                                     lhsT=w3_w[b][:, P * m : P * (m + 1)].bitcast(E4M3), lhsT_scale=w3_s[b][:, P * m : P * (m + 1)],
                                     rhs=x_w[b][:, lane_cols].bitcast(E4M3), rhs_scale=x_s[b][:, lane_cols],
-                                    start=False, stop=(b == 1 and m == 3))
+                                    start=False, stop=(b == 1 and closes[c][m]))
 
         for c in range(4):
             lane_cols = slice(P * c, P * (c + 1))
             for m in range(4):
                 for a in range(2):
-                    nc.tensor.matmul_mx(out=scores[c][:, m, :],
+                    nc.tensor.matmul_mx(out=scores[c][m],
                                         lhsT=w4_w[:, a, 2 * P * m : 2 * P * (m + 1)].bitcast(E2M1), lhsT_scale=w4_s[:, a, P * m : P * (m + 1)],
                                         rhs=v_w[a][:, lane_cols].bitcast(E4M3), rhs_scale=v_planes[a][:, lane_cols],
-                                        start=(m == 0 and a == 0), stop=False)
+                                        start=(opens[c][m] and a == 0), stop=False)
 
         for c in range(4):
             score_pass(0, c)
         out_rows = out.rearrange("(m p) j -> p m j", m=4)
 
-        def finish(c, engine):
+        def finish(c, engines):
             score_pass(1, c)
-            result = keep.tile([P, 4, P], F32, name=f"result{c}")
-            copy_on(engine, result[:], scores[c])
-            nc.sync.dma_start(out=out_rows[:, :, P * c : P * (c + 1)], in_=result[:])
+            first = 0
+            for (bank, count), engine in zip(homes[c], engines):
+                result = keep.tile([P, count, P], F32, name=f"result{bank}")
+                copy_on(engine, result[:], banks[bank][:, : P * count].rearrange("p (m j) -> p m j", m=count))
+                queue = nc.scalar if (c == 3 and engine == "scalar") else nc.sync
+                queue.dma_start(out=out_rows[:, first : first + count, P * c : P * (c + 1)], in_=result[:])
+                first = first + count
 
         picked = gather_x(1, 0, HALF, "late0")
         third = gather_x(1, HALF, P, "late1")
         quantize_x(1, 0, HALF, "scalar", picked, "tail")
-        finish(0, "scalar")
-        finish(1, "scalar")
+        finish(0, ["scalar"])
+        finish(1, ["scalar"])
         fourth = gather_x(1, HALF + P, P, "tail")
         quantize_x(1, HALF, P, "scalar", third)
-        finish(2, "scalar")
+        finish(2, ["scalar"])
         quantize_x(1, HALF + P, P, "vector", fourth)
-        finish(3, "vector")
+        finish(3, ["scalar", "vector"])

import math
from contextlib import ExitStack

import concourse.mybir as mybir
from concourse.masks import make_identity

K, T, S, H, T2, N = 1024, 2048, 512, 1024, 1024, 512
FLOPS = 2 * K * H * S * 2 + 2 * H * N * S + 2 * K * N * S

F32 = mybir.dt.float32
BF16 = mybir.dt.bfloat16
I32 = mybir.dt.int32
U32 = mybir.dt.uint32
U16 = mybir.dt.uint16
U8 = mybir.dt.uint8
E4M3 = mybir.dt.float8_e4m3fn_x4
E2M1 = mybir.dt.float4_e2m1fn_x4
ACT = mybir.ActivationFunctionType
ALU = mybir.AluOpType

P = 128
PACK = 4
KP = P * PACK
HALF = S // 2
ROUNDER = 1.5 * 2.0**23


def tile_list_interference_lane_scores_kernel(
    tc, tab_words, tab_scales, offs, w1, w2_words, w2_scales, phase, gain,
    page0, wgs, offs2, wgt, offs3, w3, w4_words, w4_scales, out,
):
    nc = tc.nc
    with ExitStack() as ctx:
        keep = ctx.enter_context(tc.tile_pool(name="keep", bufs=1))
        stage = ctx.enter_context(tc.tile_pool(name="stage", bufs=4))
        rounded = ctx.enter_context(tc.tile_pool(name="rounded", bufs=3))
        psum = ctx.enter_context(tc.psum_pool(name="psum", bufs=1))

        def held(shape, dtype, name):
            return keep.tile(shape, dtype, name=name, align_bytes=64)

        picks = keep.tile([P, S // 16], U16, name="picks")
        cells = keep.tile([P, S // 16], U16, name="cells")
        lanes = keep.tile([P, S // 16], U16, name="lanes")

        tab_w = [held([P, T], U32, f"tab_w{a}") for a in range(2)]
        tab_s = held([P, T], U8, "tab_s")
        v_w = [held([P, S], U32, f"v_w{a}") for a in range(2)]
        v_s = held([P, S], U8, "v_s")
        v_s1 = held([P, S], U8, "v_s1")
        w2_s_raw = held([P, H], U8, "w2_s_raw")
        w2_s = held([P, H], U8, "w2_s")
        w2_w = [held([P, 2, KP], U32, f"w2_w{b}") for b in range(2)]
        w1_w = [[held([P, KP], U32, f"w1_w{b}{a}") for a in range(2)] for b in range(2)]
        w1_s = [[held([P, KP], U8, f"w1_s{b}{a}") for a in range(2)] for b in range(2)]
        w3_w = [held([P, N], U32, f"w3_w{b}") for b in range(2)]
        w3_s = [held([P, N], U8, f"w3_s{b}") for b in range(2)]
        w4_w = held([P, 2, 2 * N], U8, "w4_w")
        w4_s = held([P, 2, N], U8, "w4_s")
        phase_sb = held([P, 2, PACK], F32, "phase_sb")
        phase_turns = held([P, 2, PACK], F32, "phase_turns")
        gain_sb = held([P, 2, PACK], F32, "gain_sb")
        wgs_sb = held([P, PACK * S], F32, "wgs_sb")
        wgt_sb = held([P, S], F32, "wgt_sb")
        page = [[held([P, T2], F32, f"page{b}{i}") for i in range(PACK)] for b in range(2)]

        nc.vector.memset(tab_s[:].bitcast(I32), 0)
        nc.vector.memset(w2_s_raw[:].bitcast(I32), 0)
        nc.gpsimd.memset(w4_s[:].rearrange("p a n -> p (a n)").bitcast(I32), 0)
        nc.gpsimd.memset(v_s1[:].bitcast(I32), 0)

        def load_tab_words(a):
            nc.sync.dma_start(out=tab_w[a][:].bitcast(I32),
                              in_=tab_words[a].rearrange("p t i -> p (t i)").bitcast(I32))

        def load_packed_scales(queue, tile, scales, q):
            queue.dma_start(out=tile[32 * q : 32 * q + 8, :].bitcast(I32),
                              in_=scales[:, 4 * q : 4 * q + 4, :].bitcast(I32))

        def load_w2_words(b):
            raw = keep.tile([P, 2, KP], U32, name=f"w2_raw{b}", align_bytes=64)
            src = w2_words.rearrange("a p c i -> p a (c i)")[:, :, PACK * KP * b : PACK * KP * (b + 1)]
            nc.sync.dma_start(out=raw[:].bitcast(I32), in_=src.bitcast(I32))
            return raw

        def load_rows(w, a, cols):
            raw = stage.tile([P, PACK, KP], F32, name="raw", tag="raw")
            nc.sync.dma_start(out=raw[:], in_=w[KP * a : KP * (a + 1), cols].rearrange("(p j) c -> p j c", j=PACK))
            return raw

        page_rows = page0.rearrange("(b p i) c -> b i p c", b=2, i=PACK)

        def load_page(b, i):
            nc.sync.dma_start(out=page[b][i][:], in_=page_rows[b, i])

        def deal_w2(b, raw):
            nc.vector.tensor_copy(
                out=w2_w[b][:].bitcast(I32).rearrange("p a (t g m) -> p a g t m", t=PACK, m=4),
                in_=raw[:].bitcast(I32).rearrange("p a (g m t) -> p a g t m", t=PACK, m=4))

        def copy_on(engine, out, in_):
            if engine == "vector":
                nc.vector.tensor_copy(out=out, in_=in_)
            else:
                nc.scalar.copy(out=out, in_=in_)

        def quantize(codes, scales, grouped):
            nc.vector.quantize_mx(out=codes.bitcast(E4M3), scales=scales, in_=grouped)

        def grouped_tile(width, tag):
            if tag is None:
                return rounded.tile([P, PACK * width], BF16, name="grouped", tag="grouped", align_bytes=64)
            return keep.tile([P, PACK * width], BF16, name="grouped", tag=tag, align_bytes=64)

        def round_w1(engines, raw, tag=None):
            grouped = grouped_tile(KP, tag)
            first = 0
            for engine, share in engines:
                copy_on(engine, grouped[:].rearrange("p (t m j) -> p m j t", t=PACK, j=PACK)[:, first : first + share],
                        raw[:].rearrange("p j (m t) -> p m j t", t=PACK)[:, first : first + share])
                first = first + share
            return grouped

        def round_rows(engine, raw, width, tag=None):
            grouped = grouped_tile(width, tag)
            copy_on(engine, grouped[:].rearrange("p (c i t) -> p c t i", i=4, t=PACK),
                    raw.rearrange("p t (c i) -> p c t i", i=4))
            return grouped

        banks = [psum.tile([P, S], F32, name=f"bank{n}") for n in range(8)]

        def first_product(bank, lhs_w, lhs_s):
            acc = banks[bank]
            for a in range(2):
                nc.tensor.matmul_mx(out=acc[:], lhsT=lhs_w(a).bitcast(E4M3), lhsT_scale=lhs_s(a),
                                    rhs=v_w[a][:].bitcast(E4M3), rhs_scale=v_s[4 * a :, :],
                                    start=(a == 0), stop=(a == 1))
            return acc

        turns = [keep.tile([P, 2 * S], F32, name="turns", tag=f"turns{n}", align_bytes=64) for n in range(2)]
        whole = keep.tile([P, PACK * S], U32, name="whole")
        ring = [keep.tile([P, 2 * S], F32, name=f"ring{n}") for n in range(4)]
        sine = [keep.tile([P, PACK * S], F32, name=f"sine{b}") for b in range(2)]

        def slot(tile_, i, count=1):
            return tile_[:, S * i : S * (i + count)]

        def phase_in_turns(b, i, bank):
            cols = slice(P * i, P * (i + 1))
            acc = first_product(bank, lambda a: w2_w[b][:, a, cols],
                                lambda a: w2_s[4 * a :, KP * b + P * i : KP * b + P * (i + 1)])
            nc.scalar.activation(out=slot(turns[i // 2], i % 2), in_=acc[:], func=ACT.Identity,
                                 scale=1.0 / (2.0 * math.pi), bias=phase_turns[:, b, i : i + 1])

        def drop_whole_turns(i, count, engine, home):
            if engine == "vector":
                nc.vector.tensor_scalar(out=slot(whole, i, count).bitcast(I32), in0=slot(turns[i // 2], i % 2, count),
                                        scalar1=ROUNDER, scalar2=None, op0=ALU.add)
            else:
                nc.scalar.activation(out=slot(whole, i, count), in_=slot(turns[i // 2], i % 2, count), func=ACT.Copy, bias=ROUNDER)
            nc.vector.scalar_tensor_tensor(out=home, in0=slot(whole, i, count).bitcast(I32), scalar=ROUNDER,
                                           in1=slot(turns[i // 2], i % 2, count), op0=ALU.subtract, op1=ALU.subtract)
            return home

        def reduce_pair(b, pair, first_bank, home):
            for i in (2 * pair, 2 * pair + 1):
                phase_in_turns(b, i, first_bank + i % 2)
            return drop_whole_turns(2 * pair, 2, "scalar", home)

        def take_sine(b, i, count, rest):
            nc.scalar.activation(out=slot(sine[b], i, count), in_=rest, func=ACT.Sin, scale=-2.0 * math.pi)

        def make_factor(b, i, home):
            nc.vector.scalar_tensor_tensor(out=home, in0=slot(sine[b], i), scalar=gain_sb[:, b, i : i + 1],
                                           in1=slot(wgs_sb, i), op0=ALU.mult, op1=ALU.mult)
            return home

        def amplitude(b, i, bank, home):
            cols = slice(P * i, P * (i + 1))
            acc = first_product(bank, lambda a: w1_w[b][a][:, cols], lambda a: w1_s[b][a][:, cols])
            nc.scalar.activation(out=home, in_=acc[:], func=ACT.Exp)
            return home

        def replace_cells(b, i, amp, factor):
            nc.vector.tensor_tensor(page[b][i][:].indirect(cells[:]), amp, factor, ALU.mult)

        def gather_x(b, first, width, tag):
            picked = keep.tile([P, PACK, width], F32, name="picked", tag=tag, align_bytes=64)
            for i in range(PACK):
                nc.vector.tensor_tensor(picked[:, i, :], page[b][i][:].indirect(lanes[:, first // 16 : (first + width) // 16]),
                                        wgt_sb[:, first : first + width], ALU.mult)
            return picked

        identity = held([P, P], F32, "identity")
        make_identity(nc, identity[:])
        wgs_raw = held([P, S], F32, "wgs_raw")
        nc.sync.dma_start(out=wgs_raw[:], in_=wgs)
        nc.sync.dma_start(picks[:], offs)
        load_tab_words(0)
        for q in range(4):
            load_packed_scales(nc.sync, tab_s, tab_scales, q)
        load_tab_words(1)
        nc.scalar.dma_start(out=phase_sb[:], in_=phase.rearrange("(b p i) -> p b i", b=2, i=PACK))
        for q in range(4):
            load_packed_scales(nc.sync, w2_s_raw, w2_scales, q)
        w2_raw = load_w2_words(0)
        w1_raw = [load_rows(w1, a, slice(0, KP)) for a in range(2)]
        nc.scalar.dma_start(out=gain_sb[:], in_=gain.rearrange("(b p i) -> p b i", b=2, i=PACK))

        for c in range(4):
            nc.tensor.transpose(banks[7][:, P * c : P * (c + 1)], wgs_raw[:, P * c : P * (c + 1)], identity[:])
        wgs_turned = held([P, PACK, S], F32, "wgs_turned")
        by_slot = banks[7][:].rearrange("p (c m i) -> p i c m", c=4, i=PACK)
        for i, bank in enumerate([0, 1, 4, 5]):
            nc.scalar.copy(out=wgs_turned[:, i, :].rearrange("p (c q m) -> p c q m", c=4, q=4),
                           in_=by_slot[:, i].unsqueeze(2).broadcast_to([P, 4, 4, 32]))
            for c in range(4):
                nc.tensor.transpose(banks[bank][:, P * c : P * (c + 1)], wgs_turned[:, i, P * c : P * (c + 1)], identity[:])
            nc.scalar.copy(out=slot(wgs_sb, i), in_=banks[bank][:])

        nc.vector.tensor_copy(v_w[0][:], tab_w[0][:].indirect(picks[:]))
        nc.vector.tensor_copy(v_s[:], tab_s[:].indirect(picks[:]))
        nc.vector.tensor_copy(v_w[1][:], tab_w[1][:].indirect(picks[:]))
        nc.vector.tensor_copy(out=w2_s[:].rearrange("p (b t m) -> p b t m", b=2, t=PACK),
                              in_=w2_s_raw[:].rearrange("p (b m t) -> p b t m", b=2, t=PACK))
        deal_w2(0, w2_raw)
        nc.sync.dma_start(cells[:], offs2)
        load_page(0, 0)
        w2_raw = load_w2_words(1)
        nc.scalar.activation(out=phase_turns[:], in_=phase_sb[:], func=ACT.Copy, scale=1.0 / (2.0 * math.pi))
        for i in range(2):
            phase_in_turns(0, i, 2 + i)
            take_sine(0, i, 1, drop_whole_turns(i, 1, "vector", slot(ring[i], 0)))
        for a, engines in enumerate([[("vector", P)], [("scalar", 48), ("vector", 80)]]):
            quantize(w1_w[0][a][:], w1_s[0][a][:], round_w1(engines, w1_raw[a], [None, "turns0"][a])[:])
        first_home = keep.tile([P, S], F32, name="first_home")
        factor = [make_factor(0, 0, first_home[:]), make_factor(0, 1, slot(ring[1], 1))]

        for i in range(1, PACK):
            load_page(0, i)
        w1_raw = [load_rows(w1, a, slice(KP, H)) for a in range(2)]
        nc.sync.dma_start(lanes[:], offs3)
        nc.sync.dma_start(out=wgt_sb[:], in_=wgt)
        nc.sync.dma_start(out=w4_w[:].bitcast(I32), in_=w4_words.rearrange("a p c -> p a c").bitcast(I32))
        for q in range(4):
            nc.sync.dma_start(out=w4_s[32 * q : 32 * q + 4].bitcast(I32),
                              in_=w4_scales[:, 4 * q : 4 * q + 4, :].rearrange("a q n -> q a n").bitcast(I32))
        for q in range(4):
            nc.sync.dma_start(out=v_s1[32 * q : 32 * q + 4, :].bitcast(I32), in_=v_s[32 * q + 4 : 32 * q + 8, :].bitcast(I32))
        for i in range(PACK):
            load_page(1, i)
        w3_raw = [load_rows(w3, b, slice(0, N)) for b in range(2)]

        amp_homes = [slot(ring[1], 0), slot(ring[0], 1), slot(ring[2], 0), slot(ring[3], 0)]
        amp = [amplitude(0, i, i, amp_homes[i]) for i in range(PACK)]
        replace_cells(0, 0, amp[0], factor[0])
        deal_w2(1, w2_raw)
        replace_cells(0, 1, amp[1], factor[1])
        take_sine(0, 2, 2, reduce_pair(0, 1, 0, ring[0][:]))
        turns = [keep.tile([P, 2 * S], F32, name="turns", tag="turns0", align_bytes=64), turns[1]]
        take_sine(1, 0, 2, reduce_pair(1, 0, 4, ring[1][:]))
        factor = [make_factor(0, i, slot(ring[i], 1)) for i in (2, 3)]
        replace_cells(0, 2, amp[2], factor[0])
        take_sine(1, 2, 2, reduce_pair(1, 1, 6, ring[2][:]))
        replace_cells(0, 3, amp[3], factor[1])
        factor = [make_factor(1, i, slot(ring[3 - 3 * (i // 2)], i % 2)) for i in range(PACK)]
        for a in range(2):
            quantize(w1_w[1][a][:], w1_s[1][a][:], round_w1([("scalar", P)], w1_raw[a], f"late{a}")[:])
        picked0 = [gather_x(0, HALF * h, HALF, f"late{h}") for h in range(2)]
        amp = [amplitude(1, i, i % 2, slot(ring[2 - i // 2], i % 2)) for i in range(PACK)]
        for i in range(PACK):
            replace_cells(1, i, amp[i], factor[i])
        x_w = [held([P, S], U32, f"x_w{b}") for b in range(2)]
        x_s = [held([P, S], U8, f"x_s{b}") for b in range(2)]

        def quantize_x(b, first, width, engine, picked, tag=None):
            lane_cols = slice(first, first + width)
            quantize(x_w[b][:, lane_cols], x_s[b][:, lane_cols], round_rows(engine, picked[:], width, tag)[:])

        quantize_x(0, 0, HALF, "scalar", picked0[0])
        quantize_x(0, HALF, HALF, "scalar", picked0[1])
        for b, tag in enumerate([None, "late0"]):
            quantize(w3_w[b][:], w3_s[b][:], round_rows("scalar", w3_raw[b][:], N, tag)[:])

        homes = [[(4, 4)], [(5, 4)], [(6, 4)], [(7, 2), (3, 2)]]
        scores = [[banks[bank][:, P * m : P * (m + 1)] for bank, count in homes[c] for m in range(count)] for c in range(4)]
        opens = [[m == 0 for bank, count in homes[c] for m in range(count)] for c in range(4)]
        closes = [[m == count - 1 for bank, count in homes[c] for m in range(count)] for c in range(4)]
        v_planes = [v_s, v_s1]
        def score_pass(b, c):
            lane_cols = slice(P * c, P * (c + 1))
            for m in range(4):
                nc.tensor.matmul_mx(out=scores[c][m],
                                    lhsT=w3_w[b][:, P * m : P * (m + 1)].bitcast(E4M3), lhsT_scale=w3_s[b][:, P * m : P * (m + 1)],
                                    rhs=x_w[b][:, lane_cols].bitcast(E4M3), rhs_scale=x_s[b][:, lane_cols],
                                    start=False, stop=(b == 1 and closes[c][m]))

        for c in range(4):
            lane_cols = slice(P * c, P * (c + 1))
            for m in range(4):
                for a in range(2):
                    nc.tensor.matmul_mx(out=scores[c][m],
                                        lhsT=w4_w[:, a, 2 * P * m : 2 * P * (m + 1)].bitcast(E2M1), lhsT_scale=w4_s[:, a, P * m : P * (m + 1)],
                                        rhs=v_w[a][:, lane_cols].bitcast(E4M3), rhs_scale=v_planes[a][:, lane_cols],
                                        start=(opens[c][m] and a == 0), stop=False)

        for c in range(4):
            score_pass(0, c)
        out_rows = out.rearrange("(m p) j -> p m j", m=4)

        def finish(c, engines):
            score_pass(1, c)
            first = 0
            for (bank, count), engine in zip(homes[c], engines):
                result = keep.tile([P, count, P], F32, name=f"result{bank}")
                copy_on(engine, result[:], banks[bank][:, : P * count].rearrange("p (m j) -> p m j", m=count))
                queue = nc.scalar if (c == 3 and engine == "scalar") else nc.sync
                queue.dma_start(out=out_rows[:, first : first + count, P * c : P * (c + 1)], in_=result[:])
                first = first + count

        picked = gather_x(1, 0, HALF, "late0")
        third = gather_x(1, HALF, P, "late1")
        quantize_x(1, 0, HALF, "scalar", picked, "tail")
        finish(0, ["scalar"])
        finish(1, ["scalar"])
        fourth = gather_x(1, HALF + P, P, "tail")
        quantize_x(1, HALF, P, "scalar", third)
        finish(2, ["scalar"])
        quantize_x(1, HALF + P, P, "vector", fourth)
        finish(3, ["scalar", "vector"])
